import numpy as np
import ml_dtypes


def mxq(x, axis, fmt="e4m3"):
    dtype, down = {"e4m3": (ml_dtypes.float8_e4m3fn, 7), "e5m2": (ml_dtypes.float8_e5m2, 14)}[fmt]
    v = np.moveaxis(np.asarray(x, np.float32).astype(ml_dtypes.bfloat16).astype(np.float64), axis, -1)
    blocks = v.reshape(v.shape[:-1] + (-1, 32))
    amax = np.abs(blocks).max(-1, keepdims=True)
    byte = np.maximum(np.where(amax > 0, np.frexp(amax)[1] - 1 + 127, 0) - down, 1)
    scale = np.exp2(byte - 127.0)
    codes = (blocks / scale).astype(np.float32).astype(dtype).astype(np.float64)
    return np.moveaxis((codes * scale).reshape(v.shape), -1, axis)


WIDE = False


def mx_kscale(k):
    if not WIDE:
        return np.ones(k)
    levels = np.array([10, -10, 5, -5, 0])
    if k % 512:
        return np.exp2(np.random.permutation(np.resize(levels, k // 32))).repeat(32)
    a = np.empty((k // 512, 16))
    for p in range(k // 512):
        a[p, :8] = np.random.permutation(np.resize(levels, 8))
        for g in range(8):
            far = levels[np.abs(levels - a[p, g]) >= 10]
            a[p, g + 8] = far[np.random.randint(len(far))]
    return np.exp2(a.ravel()).repeat(32)


def f64(x):
    return np.asarray(x).astype(np.float64)


def striped(idx):
    return np.tile(idx.reshape(-1, 16).T, (8, 1)).astype(np.uint16)


def unstriped(offs):
    return offs[:16].T.reshape(-1).astype(np.int64)


K, T, E, C, N = 1024, 2048, 8, 256, 256


def by_expert(wq, xq):
    return np.concatenate([wq[e].T @ xq[:, e * C:(e + 1) * C] for e in range(E)], axis=1)


def setup_inputs():
    n = np.random.standard_normal
    s = mx_kscale(K)[:, None]
    return {
        "xT": (n((K, T)) * s).astype(np.float32),
        "w": (n((E, K, N)) / np.sqrt(K) / s[None]).astype(np.float32),
        "gate": np.tile(np.random.uniform(0.2, 1.0, E * C), (N, 1)).astype(np.float32),
        "offs": striped(np.random.permutation(T)[:E * C]),
    }


def reference(xT, w, gate, offs):
    idx = unstriped(offs)
    xq = mxq(f64(xT)[:, idx], 0, "e4m3")
    y = by_expert(mxq(f64(w), 1, "e4m3"), xq)
    out = np.zeros((N, T))
    out[:, idx] = f64(gate) * y
    return out

@@ -1,0 +1,157 @@
+from contextlib import ExitStack
+
+import concourse.mybir as mybir
+from concourse.masks import make_identity
+
+K, T, E, C, N = 1024, 2048, 8, 256, 256
+FLOPS = 2 * K * N * E * C
+BYTES = 4 * (K * T + E * K * N + E * C + N * T) + 2 * 128 * 128
+
+F32 = mybir.dt.float32
+BF16 = mybir.dt.bfloat16
+U32 = mybir.dt.uint32
+U16 = mybir.dt.uint16
+U8 = mybir.dt.uint8
+FP8X4 = mybir.dt.float8_e4m3fn_x4
+COPY = mybir.ActivationFunctionType.Copy
+MULT = mybir.AluOpType.mult
+ADD = mybir.AluOpType.add
+
+P = 128
+PASSES = K // 512
+CHUNK = 512
+X_SCALAR = 256
+W_SCALAR = 160
+
+
+def tile_routed_moe_kernel(tc, xT, w, gate, offs, out):
+    nc = tc.nc
+    x_rows = xT.rearrange("(g p j) t -> g p j t", p=P, j=4)
+    w_rows = w.rearrange("e (g p j) n -> e p g j n", p=P, j=4)
+
+    with ExitStack() as ctx:
+        keep = ctx.enter_context(tc.tile_pool(name="keep", bufs=1))
+        raws = ctx.enter_context(tc.tile_pool(name="raws", bufs=12))
+        groups = ctx.enter_context(tc.tile_pool(name="groups", bufs=3))
+        wq = ctx.enter_context(tc.tile_pool(name="wq", bufs=4))
+        ys = ctx.enter_context(tc.tile_pool(name="ys", bufs=3))
+        psum_y = ctx.enter_context(tc.psum_pool(name="psum_y", bufs=3))
+        psum_t = ctx.enter_context(tc.psum_pool(name="psum_t", bufs=3))
+        psum_g = ctx.enter_context(tc.psum_pool(name="psum_g", bufs=1))
+
+        offsets = keep.tile([P, E * C // 16], U16)
+        x_codes = [keep.tile([P, T], U32, name=f"x_codes{g}", align_bytes=64) for g in range(PASSES)]
+        x_bytes = keep.tile([P, T], U8, align_bytes=64)
+        s_codes = [keep.tile([P, E * C], U32, name=f"s_codes{g}", align_bytes=64) for g in range(PASSES)]
+        s_bytes = keep.tile([P, E * C], U8, align_bytes=64)
+        window = [keep.tile([P, T], F32, name=f"window{h}") for h in range(2)]
+        ident = keep.tile([P, P], F32)
+        gate_rows = keep.tile([P, P], F32)
+        gate_cols = keep.tile([P, 16], F32)
+
+        nc.gpsimd.memset(x_bytes[:], 0)
+        nc.gpsimd.memset(gate_rows[:], 0.0)
+        make_identity(nc, ident[:])
+
+        x_raw = {}
+        w_raw = {}
+        for g in range(PASSES):
+            for c in range(T // CHUNK):
+                raw = raws.tile([P, 4, CHUNK], F32, tag="raw", name="x_raw")
+                nc.sync.dma_start(raw[:], x_rows[g, :, :, c * CHUNK : (c + 1) * CHUNK])
+                x_raw[g, c] = raw
+                if g == 0 and c == 0:
+                    nc.sync.dma_start(offsets[:], offs)
+                if g == 0 and c == 1:
+                    nc.sync.dma_start(gate_rows[0:16, :], gate[0:1, :].rearrange("a (c p) -> (a c) p", p=P))
+        for e in range(E):
+            raw = raws.tile([P, PASSES, 4, N], F32, tag="raw", name="w_raw")
+            nc.sync.dma_start(raw[:], w_rows[e])
+            w_raw[e] = raw
+
+        gate_t = psum_g.tile([P, P], F32)
+        nc.tensor.transpose(gate_t[:], gate_rows[:], ident[:])
+        nc.scalar.copy(gate_cols[:], gate_t[:, 0:16])
+
+        def x_group(g, c):
+            grouped = groups.tile([P, CHUNK, 4], BF16, name="x_grouped", align_bytes=64)
+            source = x_raw[g, c][:].rearrange("p j t -> p t j")
+            nc.scalar.copy(grouped[:, 0:X_SCALAR, :], source[:, 0:X_SCALAR, :])
+            nc.vector.tensor_copy(grouped[:, X_SCALAR:, :], source[:, X_SCALAR:, :])
+            return grouped
+
+        def x_quantise(g, c, grouped):
+            cols = slice(c * CHUNK, (c + 1) * CHUNK)
+            nc.vector.quantize_mx(
+                out=x_codes[g][:, cols].bitcast(FP8X4),
+                scales=x_bytes[4 * g : P, cols],
+                in_=grouped[:].rearrange("p t j -> p (t j)"),
+            )
+
+        for g in range(PASSES):
+            for c in range(T // CHUNK):
+                x_quantise(g, c, x_group(g, c))
+            if g == 0:
+                for a in range(2):
+                    nc.vector.tensor_copy(
+                        s_codes[0][:, a * 1024 : (a + 1) * 1024],
+                        x_codes[0][:].indirect(offsets[:, a * 64 : (a + 1) * 64]),
+                    )
+
+        w_codes = {}
+        w_bytes = {}
+
+        def w_prepare(e):
+            grouped = groups.tile([P, PASSES, N, 4], BF16, name="w_grouped", align_bytes=64)
+            source = w_raw[e][:].rearrange("p g j n -> p g n j")
+            nc.scalar.copy(grouped[:, :, 0:W_SCALAR, :], source[:, :, 0:W_SCALAR, :])
+            nc.gpsimd.tensor_scalar(grouped[:, :, W_SCALAR:, :], source[:, :, W_SCALAR:, :], 1.0, 0.0, MULT, ADD)
+            codes = wq.tile([P, PASSES, N], U32, name="w_codes", align_bytes=64)
+            planes = wq.tile([P, PASSES, N], U8, name="w_bytes", align_bytes=64)
+            nc.vector.quantize_mx(
+                out=codes[:].rearrange("p g n -> p (g n)").bitcast(FP8X4),
+                scales=planes[:].rearrange("p g n -> p (g n)"),
+                in_=grouped[:].rearrange("p g n j -> p (g n j)"),
+            )
+            w_codes[e] = codes
+            w_bytes[e] = planes
+
+        def multiply(e):
+            acc = psum_y.tile([P, 2, N], F32, name="acc")
+            for s in range(2):
+                slots = slice(e * C + s * P, e * C + (s + 1) * P)
+                for g in range(PASSES):
+                    nc.tensor.matmul_mx(
+                        out=acc[:, s, :],
+                        lhsT=s_codes[g][:, slots].bitcast(FP8X4),
+                        lhsT_scale=s_bytes[4 * g : P, slots],
+                        rhs=w_codes[e][:, g, :].bitcast(FP8X4),
+                        rhs_scale=w_bytes[e][:, g, :],
+                        start=(g == 0),
+                        stop=(g == PASSES - 1),
+                    )
+            y = ys.tile([P, 2, N], F32, name="y")
+            for s in range(2):
+                nc.scalar.activation(y[:, s, :], acc[:, s, :], COPY, scale=gate_cols[:, 2 * e + s : 2 * e + s + 1])
+            return y
+
+        def turn(y, pair_y, i):
+            yt = psum_t.tile([P, 2, 2 * P], F32, name="yt")
+            for h in range(2):
+                for s in range(2):
+                    nc.tensor.transpose(yt[:, h, s * P : (s + 1) * P], y[:, s, h * P : (h + 1) * P], ident[:])
+            nc.scalar.copy(pair_y[:, :, i * C : (i + 1) * C], yt[:])
+
+        for q in range(4):
+            cols = slice(q * 512, (q + 1) * 512)
+            list_cols = offsets[:, q * 32 : (q + 1) * 32]
+            nc.vector.tensor_copy(s_codes[1][:, cols], x_codes[1][:].indirect(list_cols))
+            nc.vector.tensor_copy(s_bytes[:, cols], x_bytes[:].indirect(list_cols))
+            pair_y = ys.tile([P, 2, 2 * C], F32, name="pair_y")
+            for i in range(2):
+                w_prepare(2 * q + i)
+                turn(multiply(2 * q + i), pair_y, i)
+            for h in range(2):
+                nc.vector.tensor_copy(window[h][:].indirect(list_cols), pair_y[:, h, :])
+        for h in range(2):
+            nc.sync.dma_start(out[h * P : (h + 1) * P, :], window[h][:])

@@ -14,14 +14,11 @@ U16 = mybir.dt.uint16
 U8 = mybir.dt.uint8
 FP8X4 = mybir.dt.float8_e4m3fn_x4
 COPY = mybir.ActivationFunctionType.Copy
-MULT = mybir.AluOpType.mult
-ADD = mybir.AluOpType.add
 
 P = 128
 PASSES = K // 512
 CHUNK = 512
-X_SCALAR = 256
-W_SCALAR = 160
+X_SCALAR = 352
 
 
 def tile_routed_moe_kernel(tc, xT, w, gate, offs, out):
@@ -32,7 +29,8 @@ def tile_routed_moe_kernel(tc, xT, w, gate, offs, out):
     with ExitStack() as ctx:
         keep = ctx.enter_context(tc.tile_pool(name="keep", bufs=1))
         raws = ctx.enter_context(tc.tile_pool(name="raws", bufs=12))
-        groups = ctx.enter_context(tc.tile_pool(name="groups", bufs=3))
+        groups = ctx.enter_context(tc.tile_pool(name="groups", bufs=4))
+        picks = ctx.enter_context(tc.tile_pool(name="picks", bufs=1))
         wq = ctx.enter_context(tc.tile_pool(name="wq", bufs=4))
         ys = ctx.enter_context(tc.tile_pool(name="ys", bufs=3))
         psum_y = ctx.enter_context(tc.psum_pool(name="psum_y", bufs=3))
@@ -42,8 +40,7 @@ def tile_routed_moe_kernel(tc, xT, w, gate, offs, out):
         offsets = keep.tile([P, E * C // 16], U16)
         x_codes = [keep.tile([P, T], U32, name=f"x_codes{g}", align_bytes=64) for g in range(PASSES)]
         x_bytes = keep.tile([P, T], U8, align_bytes=64)
-        s_codes = [keep.tile([P, E * C], U32, name=f"s_codes{g}", align_bytes=64) for g in range(PASSES)]
-        s_bytes = keep.tile([P, E * C], U8, align_bytes=64)
+        s_codes0 = keep.tile([P, E * C], U32, align_bytes=64)
         window = [keep.tile([P, T], F32, name=f"window{h}") for h in range(2)]
         ident = keep.tile([P, P], F32)
         gate_rows = keep.tile([P, P], F32)
@@ -62,22 +59,18 @@ def tile_routed_moe_kernel(tc, xT, w, gate, offs, out):
                 x_raw[g, c] = raw
                 if g == 0 and c == 0:
                     nc.sync.dma_start(offsets[:], offs)
-                if g == 0 and c == 1:
-                    nc.sync.dma_start(gate_rows[0:16, :], gate[0:1, :].rearrange("a (c p) -> (a c) p", p=P))
+        nc.sync.dma_start(gate_rows[0:16, :], gate[0:1, :].rearrange("a (c p) -> (a c) p", p=P))
         for e in range(E):
             raw = raws.tile([P, PASSES, 4, N], F32, tag="raw", name="w_raw")
             nc.sync.dma_start(raw[:], w_rows[e])
             w_raw[e] = raw
 
-        gate_t = psum_g.tile([P, P], F32)
-        nc.tensor.transpose(gate_t[:], gate_rows[:], ident[:])
-        nc.scalar.copy(gate_cols[:], gate_t[:, 0:16])
-
         def x_group(g, c):
             grouped = groups.tile([P, CHUNK, 4], BF16, name="x_grouped", align_bytes=64)
-            source = x_raw[g, c][:].rearrange("p j t -> p t j")
-            nc.scalar.copy(grouped[:, 0:X_SCALAR, :], source[:, 0:X_SCALAR, :])
-            nc.vector.tensor_copy(grouped[:, X_SCALAR:, :], source[:, X_SCALAR:, :])
+            source = x_raw[g, c][:].rearrange("p j (q i) -> p q j i", i=4)
+            target = grouped[:].rearrange("p (q i) j -> p q j i", i=4)
+            nc.scalar.copy(target[:, 0 : X_SCALAR // 4], source[:, 0 : X_SCALAR // 4])
+            nc.vector.tensor_copy(target[:, X_SCALAR // 4 :], source[:, X_SCALAR // 4 :])
             return grouped
 
         def x_quantise(g, c, grouped):
@@ -94,7 +87,7 @@ def tile_routed_moe_kernel(tc, xT, w, gate, offs, out):
             if g == 0:
                 for a in range(2):
                     nc.vector.tensor_copy(
-                        s_codes[0][:, a * 1024 : (a + 1) * 1024],
+                        s_codes0[:, a * 1024 : (a + 1) * 1024],
                         x_codes[0][:].indirect(offsets[:, a * 64 : (a + 1) * 64]),
                     )
 
@@ -103,9 +96,8 @@ def tile_routed_moe_kernel(tc, xT, w, gate, offs, out):
 
         def w_prepare(e):
             grouped = groups.tile([P, PASSES, N, 4], BF16, name="w_grouped", align_bytes=64)
-            source = w_raw[e][:].rearrange("p g j n -> p g n j")
-            nc.scalar.copy(grouped[:, :, 0:W_SCALAR, :], source[:, :, 0:W_SCALAR, :])
-            nc.gpsimd.tensor_scalar(grouped[:, :, W_SCALAR:, :], source[:, :, W_SCALAR:, :], 1.0, 0.0, MULT, ADD)
+            source = w_raw[e][:].rearrange("p g j (q i) -> p g q j i", i=4)
+            nc.scalar.copy(grouped[:].rearrange("p g (q i) j -> p g q j i", i=4), source)
             codes = wq.tile([P, PASSES, N], U32, name="w_codes", align_bytes=64)
             planes = wq.tile([P, PASSES, N], U8, name="w_bytes", align_bytes=64)
             nc.vector.quantize_mx(
@@ -116,15 +108,16 @@ def tile_routed_moe_kernel(tc, xT, w, gate, offs, out):
             w_codes[e] = codes
             w_bytes[e] = planes
 
-        def multiply(e):
+        def multiply(e, codes1, planes):
             acc = psum_y.tile([P, 2, N], F32, name="acc")
             for s in range(2):
-                slots = slice(e * C + s * P, e * C + (s + 1) * P)
+                first = (e % 2) * C + s * P
                 for g in range(PASSES):
+                    codes = (s_codes0[:, e * C + s * P : e * C + (s + 1) * P], codes1[:, first : first + P])[g]
                     nc.tensor.matmul_mx(
                         out=acc[:, s, :],
-                        lhsT=s_codes[g][:, slots].bitcast(FP8X4),
-                        lhsT_scale=s_bytes[4 * g : P, slots],
+                        lhsT=codes.bitcast(FP8X4),
+                        lhsT_scale=planes[4 * g : P, first : first + P],
                         rhs=w_codes[e][:, g, :].bitcast(FP8X4),
                         rhs_scale=w_bytes[e][:, g, :],
                         start=(g == 0),
@@ -142,16 +135,36 @@ def tile_routed_moe_kernel(tc, xT, w, gate, offs, out):
                     nc.tensor.transpose(yt[:, h, s * P : (s + 1) * P], y[:, s, h * P : (h + 1) * P], ident[:])
             nc.scalar.copy(pair_y[:, :, i * C : (i + 1) * C], yt[:])
 
-        for q in range(4):
-            cols = slice(q * 512, (q + 1) * 512)
+        gate_t = psum_g.tile([P, P], F32)
+        nc.tensor.transpose(gate_t[:], gate_rows[:], ident[:])
+        nc.scalar.copy(gate_cols[:], gate_t[:, 0:16])
+
+        def pick(q):
             list_cols = offsets[:, q * 32 : (q + 1) * 32]
-            nc.vector.tensor_copy(s_codes[1][:, cols], x_codes[1][:].indirect(list_cols))
-            nc.vector.tensor_copy(s_bytes[:, cols], x_bytes[:].indirect(list_cols))
+            codes = picks.tile([P, 512], U32, name="s_codes1", align_bytes=64)
+            planes = picks.tile([P, 512], U8, name="s_bytes", align_bytes=64)
+            nc.vector.tensor_copy(codes[:], x_codes[1][:].indirect(list_cols))
+            nc.vector.tensor_copy(planes[:], x_bytes[:].indirect(list_cols))
+            return codes, planes
+
+        def put_back(q, pair_y):
+            for h in range(2):
+                nc.vector.tensor_copy(window[h][:].indirect(offsets[:, q * 32 : (q + 1) * 32]), pair_y[:, h, :])
+
+        w_prepare(0)
+        w_prepare(1)
+        picked = pick(0)
+        for q in range(4):
+            sums = []
+            for i in range(2):
+                sums.append(multiply(2 * q + i, *picked))
+                if q < 3:
+                    w_prepare(2 * q + 2 + i)
+            if q < 3:
+                picked = pick(q + 1)
             pair_y = ys.tile([P, 2, 2 * C], F32, name="pair_y")
             for i in range(2):
-                w_prepare(2 * q + i)
-                turn(multiply(2 * q + i), pair_y, i)
-            for h in range(2):
-                nc.vector.tensor_copy(window[h][:].indirect(list_cols), pair_y[:, h, :])
+                turn(sums[i], pair_y, i)
+            put_back(q, pair_y)
         for h in range(2):
             nc.sync.dma_start(out[h * P : (h + 1) * P, :], window[h][:])

@@ -1,11 +1,9 @@
 from contextlib import ExitStack
 
 import concourse.mybir as mybir
-from concourse.masks import make_identity
 
 K, T, E, C, N = 1024, 2048, 8, 256, 256
 FLOPS = 2 * K * N * E * C
-BYTES = 4 * (K * T + E * K * N + E * C + N * T) + 2 * 128 * 128
 
 F32 = mybir.dt.float32
 BF16 = mybir.dt.bfloat16
@@ -13,68 +11,67 @@ U32 = mybir.dt.uint32
 U16 = mybir.dt.uint16
 U8 = mybir.dt.uint8
 FP8X4 = mybir.dt.float8_e4m3fn_x4
-COPY = mybir.ActivationFunctionType.Copy
+MULT = mybir.AluOpType.mult
 
 P = 128
 PASSES = K // 512
-CHUNK = 512
-X_SCALAR = 352
+X_PIECES = ((512, 512, 512, 256, 256), (512, 512, 512, 256, 256))
+X_SCALAR = ((192, 192, 192, 96, 96), (448, 448, 448, 128, 160))
 
 
 def tile_routed_moe_kernel(tc, xT, w, gate, offs, out):
     nc = tc.nc
     x_rows = xT.rearrange("(g p j) t -> g p j t", p=P, j=4)
+    gate_rows = gate.rearrange("(h p) s -> p h s", p=P)
     w_rows = w.rearrange("e (g p j) n -> e p g j n", p=P, j=4)
 
     with ExitStack() as ctx:
         keep = ctx.enter_context(tc.tile_pool(name="keep", bufs=1))
-        raws = ctx.enter_context(tc.tile_pool(name="raws", bufs=12))
+        raws = ctx.enter_context(tc.tile_pool(name="raws", bufs=11))
         groups = ctx.enter_context(tc.tile_pool(name="groups", bufs=4))
-        picks = ctx.enter_context(tc.tile_pool(name="picks", bufs=1))
-        wq = ctx.enter_context(tc.tile_pool(name="wq", bufs=4))
+        w_groups = ctx.enter_context(tc.tile_pool(name="w_groups", bufs=6))
+        picks = ctx.enter_context(tc.tile_pool(name="picks", bufs=3))
+        wq = ctx.enter_context(tc.tile_pool(name="wq", bufs=8))
         ys = ctx.enter_context(tc.tile_pool(name="ys", bufs=3))
-        psum_y = ctx.enter_context(tc.psum_pool(name="psum_y", bufs=3))
-        psum_t = ctx.enter_context(tc.psum_pool(name="psum_t", bufs=3))
-        psum_g = ctx.enter_context(tc.psum_pool(name="psum_g", bufs=1))
+        psum = ctx.enter_context(tc.psum_pool(name="psum", bufs=4))
 
         offsets = keep.tile([P, E * C // 16], U16)
         x_codes = [keep.tile([P, T], U32, name=f"x_codes{g}", align_bytes=64) for g in range(PASSES)]
         x_bytes = keep.tile([P, T], U8, align_bytes=64)
         s_codes0 = keep.tile([P, E * C], U32, align_bytes=64)
         window = [keep.tile([P, T], F32, name=f"window{h}") for h in range(2)]
-        ident = keep.tile([P, P], F32)
-        gate_rows = keep.tile([P, P], F32)
-        gate_cols = keep.tile([P, 16], F32)
+        gates = keep.tile([P, 2, E * C], F32)
 
         nc.gpsimd.memset(x_bytes[:], 0)
-        nc.gpsimd.memset(gate_rows[:], 0.0)
-        make_identity(nc, ident[:])
 
         x_raw = {}
         w_raw = {}
         for g in range(PASSES):
-            for c in range(T // CHUNK):
-                raw = raws.tile([P, 4, CHUNK], F32, tag="raw", name="x_raw")
-                nc.sync.dma_start(raw[:], x_rows[g, :, :, c * CHUNK : (c + 1) * CHUNK])
-                x_raw[g, c] = raw
-                if g == 0 and c == 0:
+            start = 0
+            for i, width in enumerate(X_PIECES[g]):
+                raw = raws.tile([P, 4, width], F32, tag="raw", name="x_raw")
+                nc.sync.dma_start(raw[:], x_rows[g, :, :, start : start + width])
+                x_raw[g, i] = raw
+                start += width
+                if g == 0 and i == 0:
                     nc.sync.dma_start(offsets[:], offs)
-        nc.sync.dma_start(gate_rows[0:16, :], gate[0:1, :].rearrange("a (c p) -> (a c) p", p=P))
         for e in range(E):
+            if e in (2, 5):
+                slots = slice(0, 1024) if e == 2 else slice(1024, 2048)
+                nc.sync.dma_start(gates[:, :, slots], gate_rows[:, :, slots])
             raw = raws.tile([P, PASSES, 4, N], F32, tag="raw", name="w_raw")
             nc.sync.dma_start(raw[:], w_rows[e])
             w_raw[e] = raw
 
-        def x_group(g, c):
-            grouped = groups.tile([P, CHUNK, 4], BF16, name="x_grouped", align_bytes=64)
-            source = x_raw[g, c][:].rearrange("p j (q i) -> p q j i", i=4)
+        def x_quantise(g, i, start):
+            width = X_PIECES[g][i]
+            cut = X_SCALAR[g][i] // 4
+            grouped = groups.tile([P, width, 4], BF16, name="x_grouped", align_bytes=64)
+            source = x_raw[g, i][:].rearrange("p j (q i) -> p q j i", i=4)
             target = grouped[:].rearrange("p (q i) j -> p q j i", i=4)
-            nc.scalar.copy(target[:, 0 : X_SCALAR // 4], source[:, 0 : X_SCALAR // 4])
-            nc.vector.tensor_copy(target[:, X_SCALAR // 4 :], source[:, X_SCALAR // 4 :])
-            return grouped
-
-        def x_quantise(g, c, grouped):
-            cols = slice(c * CHUNK, (c + 1) * CHUNK)
+            nc.scalar.copy(target[:, 0:cut], source[:, 0:cut])
+            nc.vector.tensor_copy(target[:, cut:], source[:, cut:])
+            cols = slice(start, start + width)
             nc.vector.quantize_mx(
                 out=x_codes[g][:, cols].bitcast(FP8X4),
                 scales=x_bytes[4 * g : P, cols],
@@ -82,8 +79,10 @@ def tile_routed_moe_kernel(tc, xT, w, gate, offs, out):
             )
 
         for g in range(PASSES):
-            for c in range(T // CHUNK):
-                x_quantise(g, c, x_group(g, c))
+            start = 0
+            for i, width in enumerate(X_PIECES[g]):
+                x_quantise(g, i, start)
+                start += width
             if g == 0:
                 for a in range(2):
                     nc.vector.tensor_copy(
@@ -95,7 +94,7 @@ def tile_routed_moe_kernel(tc, xT, w, gate, offs, out):
         w_bytes = {}
 
         def w_prepare(e):
-            grouped = groups.tile([P, PASSES, N, 4], BF16, name="w_grouped", align_bytes=64)
+            grouped = w_groups.tile([P, PASSES, N, 4], BF16, name="w_grouped", align_bytes=64)
             source = w_raw[e][:].rearrange("p g j (q i) -> p g q j i", i=4)
             nc.scalar.copy(grouped[:].rearrange("p g (q i) j -> p g q j i", i=4), source)
             codes = wq.tile([P, PASSES, N], U32, name="w_codes", align_bytes=64)
@@ -108,37 +107,6 @@ def tile_routed_moe_kernel(tc, xT, w, gate, offs, out):
             w_codes[e] = codes
             w_bytes[e] = planes
 
-        def multiply(e, codes1, planes):
-            acc = psum_y.tile([P, 2, N], F32, name="acc")
-            for s in range(2):
-                first = (e % 2) * C + s * P
-                for g in range(PASSES):
-                    codes = (s_codes0[:, e * C + s * P : e * C + (s + 1) * P], codes1[:, first : first + P])[g]
-                    nc.tensor.matmul_mx(
-                        out=acc[:, s, :],
-                        lhsT=codes.bitcast(FP8X4),
-                        lhsT_scale=planes[4 * g : P, first : first + P],
-                        rhs=w_codes[e][:, g, :].bitcast(FP8X4),
-                        rhs_scale=w_bytes[e][:, g, :],
-                        start=(g == 0),
-                        stop=(g == PASSES - 1),
-                    )
-            y = ys.tile([P, 2, N], F32, name="y")
-            for s in range(2):
-                nc.scalar.activation(y[:, s, :], acc[:, s, :], COPY, scale=gate_cols[:, 2 * e + s : 2 * e + s + 1])
-            return y
-
-        def turn(y, pair_y, i):
-            yt = psum_t.tile([P, 2, 2 * P], F32, name="yt")
-            for h in range(2):
-                for s in range(2):
-                    nc.tensor.transpose(yt[:, h, s * P : (s + 1) * P], y[:, s, h * P : (h + 1) * P], ident[:])
-            nc.scalar.copy(pair_y[:, :, i * C : (i + 1) * C], yt[:])
-
-        gate_t = psum_g.tile([P, P], F32)
-        nc.tensor.transpose(gate_t[:], gate_rows[:], ident[:])
-        nc.scalar.copy(gate_cols[:], gate_t[:, 0:16])
-
         def pick(q):
             list_cols = offsets[:, q * 32 : (q + 1) * 32]
             codes = picks.tile([P, 512], U32, name="s_codes1", align_bytes=64)
@@ -147,24 +115,40 @@ def tile_routed_moe_kernel(tc, xT, w, gate, offs, out):
             nc.vector.tensor_copy(planes[:], x_bytes[:].indirect(list_cols))
             return codes, planes
 
-        def put_back(q, pair_y):
+        def multiply(e, codes1, planes, y):
+            acc = psum.tile([P, 2, C], F32, name="acc")
+            i = e % 2
+            moving = (s_codes0[:, e * C : (e + 1) * C], codes1[:, i * C : (i + 1) * C])
             for h in range(2):
-                nc.vector.tensor_copy(window[h][:].indirect(offsets[:, q * 32 : (q + 1) * 32]), pair_y[:, h, :])
+                for g in range(PASSES):
+                    nc.tensor.matmul_mx(
+                        out=acc[:, h, :],
+                        lhsT=w_codes[e][:, g, h * P : (h + 1) * P].bitcast(FP8X4),
+                        lhsT_scale=w_bytes[e][:, g, h * P : (h + 1) * P],
+                        rhs=moving[g].bitcast(FP8X4),
+                        rhs_scale=planes[4 * g : P, i * C : (i + 1) * C],
+                        start=(g == 0),
+                        stop=(g == PASSES - 1),
+                    )
+            nc.scalar.copy(y[:, :, i * C : (i + 1) * C], acc[:])
 
         w_prepare(0)
         w_prepare(1)
         picked = pick(0)
         for q in range(4):
-            sums = []
+            y = ys.tile([P, 2, 2 * C], F32, name="y")
             for i in range(2):
-                sums.append(multiply(2 * q + i, *picked))
-                if q < 3:
-                    w_prepare(2 * q + 2 + i)
+                multiply(2 * q + i, *picked, y)
             if q < 3:
+                w_prepare(2 * q + 2)
+                w_prepare(2 * q + 3)
                 picked = pick(q + 1)
-            pair_y = ys.tile([P, 2, 2 * C], F32, name="pair_y")
-            for i in range(2):
-                turn(sums[i], pair_y, i)
-            put_back(q, pair_y)
+            for h in range(2):
+                nc.vector.tensor_tensor(
+                    window[h][:].indirect(offsets[:, q * 32 : (q + 1) * 32]),
+                    y[:, h, :],
+                    gates[:, h, q * 512 : (q + 1) * 512],
+                    MULT,
+                )
         for h in range(2):
             nc.sync.dma_start(out[h * P : (h + 1) * P, :], window[h][:])

@@ -16,7 +16,7 @@ MULT = mybir.AluOpType.mult
 P = 128
 PASSES = K // 512
 X_PIECES = ((512, 512, 512, 256, 256), (512, 512, 512, 256, 256))
-X_SCALAR = ((192, 192, 192, 96, 96), (448, 448, 448, 128, 160))
+X_SCALAR = ((192, 192, 192, 128, 128), (448, 448, 448, 192, 128))
 
 
 def tile_routed_moe_kernel(tc, xT, w, gate, offs, out):
@@ -30,7 +30,7 @@ def tile_routed_moe_kernel(tc, xT, w, gate, offs, out):
         raws = ctx.enter_context(tc.tile_pool(name="raws", bufs=11))
         groups = ctx.enter_context(tc.tile_pool(name="groups", bufs=4))
         w_groups = ctx.enter_context(tc.tile_pool(name="w_groups", bufs=6))
-        picks = ctx.enter_context(tc.tile_pool(name="picks", bufs=3))
+        picks = ctx.enter_context(tc.tile_pool(name="picks", bufs=2))
         wq = ctx.enter_context(tc.tile_pool(name="wq", bufs=8))
         ys = ctx.enter_context(tc.tile_pool(name="ys", bufs=3))
         psum = ctx.enter_context(tc.psum_pool(name="psum", bufs=4))
@@ -55,13 +55,15 @@ def tile_routed_moe_kernel(tc, xT, w, gate, offs, out):
                 start += width
                 if g == 0 and i == 0:
                     nc.sync.dma_start(offsets[:], offs)
+        def load_gates(slots):
+            nc.sync.dma_start(gates[:, :, slots], gate_rows[:, :, slots])
+
+        load_gates(slice(0, 1024))
         for e in range(E):
-            if e in (2, 5):
-                slots = slice(0, 1024) if e == 2 else slice(1024, 2048)
-                nc.sync.dma_start(gates[:, :, slots], gate_rows[:, :, slots])
             raw = raws.tile([P, PASSES, 4, N], F32, tag="raw", name="w_raw")
             nc.sync.dma_start(raw[:], w_rows[e])
             w_raw[e] = raw
+        load_gates(slice(1024, 2048))
 
         def x_quantise(g, i, start):
             width = X_PIECES[g][i]
@@ -132,6 +134,15 @@ def tile_routed_moe_kernel(tc, xT, w, gate, offs, out):
                     )
             nc.scalar.copy(y[:, :, i * C : (i + 1) * C], acc[:])
 
+        def put_back(y, q, h, first, n):
+            slots = slice(q * 512 + first, q * 512 + first + n)
+            nc.vector.tensor_tensor(
+                window[h][:].indirect(offsets[:, slots.start // 16 : slots.stop // 16]),
+                y[:, h, first : first + n],
+                gates[:, h, slots],
+                MULT,
+            )
+
         w_prepare(0)
         w_prepare(1)
         picked = pick(0)
@@ -143,12 +154,12 @@ def tile_routed_moe_kernel(tc, xT, w, gate, offs, out):
                 w_prepare(2 * q + 2)
                 w_prepare(2 * q + 3)
                 picked = pick(q + 1)
-            for h in range(2):
-                nc.vector.tensor_tensor(
-                    window[h][:].indirect(offsets[:, q * 32 : (q + 1) * 32]),
-                    y[:, h, :],
-                    gates[:, h, q * 512 : (q + 1) * 512],
-                    MULT,
-                )
+                for first in (0, C):
+                    for h in range(2):
+                        put_back(y, q, h, first, C)
+            else:
+                put_back(y, q, 0, 0, C)
+                put_back(y, q, 0, C, C)
+                put_back(y, q, 1, 0, 2 * C)
         for h in range(2):
             nc.sync.dma_start(out[h * P : (h + 1) * P, :], window[h][:])

from contextlib import ExitStack

import concourse.mybir as mybir

K, T, E, C, N = 1024, 2048, 8, 256, 256
FLOPS = 2 * K * N * E * C

F32 = mybir.dt.float32
BF16 = mybir.dt.bfloat16
U32 = mybir.dt.uint32
U16 = mybir.dt.uint16
U8 = mybir.dt.uint8
FP8X4 = mybir.dt.float8_e4m3fn_x4
MULT = mybir.AluOpType.mult

P = 128
PASSES = K // 512
X_PIECES = ((512, 512, 512, 256, 256), (512, 512, 512, 256, 256))
X_SCALAR = ((192, 192, 192, 128, 128), (448, 448, 448, 192, 128))


def tile_routed_moe_kernel(tc, xT, w, gate, offs, out):
    nc = tc.nc
    x_rows = xT.rearrange("(g p j) t -> g p j t", p=P, j=4)
    gate_rows = gate.rearrange("(h p) s -> p h s", p=P)
    w_rows = w.rearrange("e (g p j) n -> e p g j n", p=P, j=4)

    with ExitStack() as ctx:
        keep = ctx.enter_context(tc.tile_pool(name="keep", bufs=1))
        raws = ctx.enter_context(tc.tile_pool(name="raws", bufs=11))
        groups = ctx.enter_context(tc.tile_pool(name="groups", bufs=4))
        w_groups = ctx.enter_context(tc.tile_pool(name="w_groups", bufs=6))
        picks = ctx.enter_context(tc.tile_pool(name="picks", bufs=2))
        wq = ctx.enter_context(tc.tile_pool(name="wq", bufs=8))
        ys = ctx.enter_context(tc.tile_pool(name="ys", bufs=3))
        psum = ctx.enter_context(tc.psum_pool(name="psum", bufs=4))

        offsets = keep.tile([P, E * C // 16], U16)
        x_codes = [keep.tile([P, T], U32, name=f"x_codes{g}", align_bytes=64) for g in range(PASSES)]
        x_bytes = keep.tile([P, T], U8, align_bytes=64)
        s_codes0 = keep.tile([P, E * C], U32, align_bytes=64)
        window = [keep.tile([P, T], F32, name=f"window{h}") for h in range(2)]
        gates = keep.tile([P, 2, E * C], F32)

        nc.gpsimd.memset(x_bytes[:], 0)

        x_raw = {}
        w_raw = {}
        for g in range(PASSES):
            start = 0
            for i, width in enumerate(X_PIECES[g]):
                raw = raws.tile([P, 4, width], F32, tag="raw", name="x_raw")
                nc.sync.dma_start(raw[:], x_rows[g, :, :, start : start + width])
                x_raw[g, i] = raw
                start += width
                if g == 0 and i == 0:
                    nc.sync.dma_start(offsets[:], offs)
        def load_gates(slots):
            nc.sync.dma_start(gates[:, :, slots], gate_rows[:, :, slots])

        load_gates(slice(0, 1024))
        for e in range(E):
            raw = raws.tile([P, PASSES, 4, N], F32, tag="raw", name="w_raw")
            nc.sync.dma_start(raw[:], w_rows[e])
            w_raw[e] = raw
        load_gates(slice(1024, 2048))

        def x_quantise(g, i, start):
            width = X_PIECES[g][i]
            cut = X_SCALAR[g][i] // 4
            grouped = groups.tile([P, width, 4], BF16, name="x_grouped", align_bytes=64)
            source = x_raw[g, i][:].rearrange("p j (q i) -> p q j i", i=4)
            target = grouped[:].rearrange("p (q i) j -> p q j i", i=4)
            nc.scalar.copy(target[:, 0:cut], source[:, 0:cut])
            nc.vector.tensor_copy(target[:, cut:], source[:, cut:])
            cols = slice(start, start + width)
            nc.vector.quantize_mx(
                out=x_codes[g][:, cols].bitcast(FP8X4),
                scales=x_bytes[4 * g : P, cols],
                in_=grouped[:].rearrange("p t j -> p (t j)"),
            )

        for g in range(PASSES):
            start = 0
            for i, width in enumerate(X_PIECES[g]):
                x_quantise(g, i, start)
                start += width
            if g == 0:
                for a in range(2):
                    nc.vector.tensor_copy(
                        s_codes0[:, a * 1024 : (a + 1) * 1024],
                        x_codes[0][:].indirect(offsets[:, a * 64 : (a + 1) * 64]),
                    )

        w_codes = {}
        w_bytes = {}

        def w_prepare(e):
            grouped = w_groups.tile([P, PASSES, N, 4], BF16, name="w_grouped", align_bytes=64)
            source = w_raw[e][:].rearrange("p g j (q i) -> p g q j i", i=4)
            nc.scalar.copy(grouped[:].rearrange("p g (q i) j -> p g q j i", i=4), source)
            codes = wq.tile([P, PASSES, N], U32, name="w_codes", align_bytes=64)
            planes = wq.tile([P, PASSES, N], U8, name="w_bytes", align_bytes=64)
            nc.vector.quantize_mx(
                out=codes[:].rearrange("p g n -> p (g n)").bitcast(FP8X4),
                scales=planes[:].rearrange("p g n -> p (g n)"),
                in_=grouped[:].rearrange("p g n j -> p (g n j)"),
            )
            w_codes[e] = codes
            w_bytes[e] = planes

        def pick(q):
            list_cols = offsets[:, q * 32 : (q + 1) * 32]
            codes = picks.tile([P, 512], U32, name="s_codes1", align_bytes=64)
            planes = picks.tile([P, 512], U8, name="s_bytes", align_bytes=64)
            nc.vector.tensor_copy(codes[:], x_codes[1][:].indirect(list_cols))
            nc.vector.tensor_copy(planes[:], x_bytes[:].indirect(list_cols))
            return codes, planes

        def multiply(e, codes1, planes, y):
            acc = psum.tile([P, 2, C], F32, name="acc")
            i = e % 2
            moving = (s_codes0[:, e * C : (e + 1) * C], codes1[:, i * C : (i + 1) * C])
            for h in range(2):
                for g in range(PASSES):
                    nc.tensor.matmul_mx(
                        out=acc[:, h, :],
                        lhsT=w_codes[e][:, g, h * P : (h + 1) * P].bitcast(FP8X4),
                        lhsT_scale=w_bytes[e][:, g, h * P : (h + 1) * P],
                        rhs=moving[g].bitcast(FP8X4),
                        rhs_scale=planes[4 * g : P, i * C : (i + 1) * C],
                        start=(g == 0),
                        stop=(g == PASSES - 1),
                    )
            nc.scalar.copy(y[:, :, i * C : (i + 1) * C], acc[:])

        def put_back(y, q, h, first, n):
            slots = slice(q * 512 + first, q * 512 + first + n)
            nc.vector.tensor_tensor(
                window[h][:].indirect(offsets[:, slots.start // 16 : slots.stop // 16]),
                y[:, h, first : first + n],
                gates[:, h, slots],
                MULT,
            )

        w_prepare(0)
        w_prepare(1)
        picked = pick(0)
        for q in range(4):
            y = ys.tile([P, 2, 2 * C], F32, name="y")
            for i in range(2):
                multiply(2 * q + i, *picked, y)
            if q < 3:
                w_prepare(2 * q + 2)
                w_prepare(2 * q + 3)
                picked = pick(q + 1)
                for first in (0, C):
                    for h in range(2):
                        put_back(y, q, h, first, C)
            else:
                put_back(y, q, 0, 0, C)
                put_back(y, q, 0, C, C)
                put_back(y, q, 1, 0, 2 * C)
        for h in range(2):
            nc.sync.dma_start(out[h * P : (h + 1) * P, :], window[h][:])
